import numpy as np
import ml_dtypes


def mxq(x, axis, fmt="e4m3"):
    dtype, down = {"e4m3": (ml_dtypes.float8_e4m3fn, 7), "e5m2": (ml_dtypes.float8_e5m2, 14)}[fmt]
    v = np.moveaxis(np.asarray(x, np.float32).astype(ml_dtypes.bfloat16).astype(np.float64), axis, -1)
    blocks = v.reshape(v.shape[:-1] + (-1, 32))
    amax = np.abs(blocks).max(-1, keepdims=True)
    byte = np.maximum(np.where(amax > 0, np.frexp(amax)[1] - 1 + 127, 0) - down, 1)
    scale = np.exp2(byte - 127.0)
    codes = (blocks / scale).astype(np.float32).astype(dtype).astype(np.float64)
    return np.moveaxis((codes * scale).reshape(v.shape), -1, axis)


WIDE = False


def mx_kscale(k):
    if not WIDE:
        return np.ones(k)
    levels = np.array([10, -10, 5, -5, 0])
    if k % 512:
        return np.exp2(np.random.permutation(np.resize(levels, k // 32))).repeat(32)
    a = np.empty((k // 512, 16))
    for p in range(k // 512):
        a[p, :8] = np.random.permutation(np.resize(levels, 8))
        for g in range(8):
            far = levels[np.abs(levels - a[p, g]) >= 10]
            a[p, g + 8] = far[np.random.randint(len(far))]
    return np.exp2(a.ravel()).repeat(32)


def f64(x):
    return np.asarray(x).astype(np.float64)


def striped(idx):
    return np.tile(idx.reshape(-1, 16).T, (8, 1)).astype(np.uint16)


def unstriped(offs):
    return offs[:16].T.reshape(-1).astype(np.int64)


def striped8(idx):
    return np.concatenate([x.reshape(-1, 16).T for x in idx]).astype(np.uint16)


def runs(offs, k):
    lists = np.stack([offs[16 * r : 16 * r + 16].T.reshape(-1) for r in range(8)]).astype(np.int64)
    return lists[np.arange(k) % 512 // 64]


def pack_weight(w):
    k, n = w.shape
    w = f64(np.asarray(w, np.float32).astype(ml_dtypes.bfloat16)).reshape(k // 32, 32, n)
    amax = np.abs(w).max(1)
    byte = np.clip(np.where(amax > 0, np.frexp(amax)[1] - 1 + 127 - 7, 1), 1, 254)
    scaled = (w * np.exp2(127.0 - byte)[:, None, :]).reshape(k, n).astype(np.float32)
    words = np.ascontiguousarray(scaled.reshape(k // 512, 128, 4, n).transpose(0, 1, 3, 2)).astype(ml_dtypes.float8_e4m3fn).view(np.uint8)
    return words, np.ascontiguousarray(byte.astype(np.uint8).reshape(k // 512, 16, n))


def unpack_weight(words, scales):
    g, p, n, _ = words.shape
    vals = np.ascontiguousarray(words).view(ml_dtypes.float8_e4m3fn).astype(np.float64) * np.repeat(np.exp2(scales.astype(np.float64) - 127.0), 8, axis=1)[..., None]
    return vals.transpose(0, 1, 3, 2).reshape(g * 512, n)


K, T, S, N, H, J = 512, 2048, 512, 512, 512, 512


def setup_inputs():
    n = np.random.standard_normal
    s = mx_kscale(K)[:, None]
    u = mx_kscale(S)
    packed_xT = pack_weight(n((K, T)) * s)
    return {
        "x_words": packed_xT[0],
        "x_scales": packed_xT[1],
        "wa": (n((K, H)) / np.sqrt(K) / s).astype(np.float32),
        "wb": (n((K, N)) / np.sqrt(K) / s).astype(np.float32),
        "tab": n((S, J)).astype(np.float32),
        "gt": (np.random.uniform(0.5, 1.5, (S, 1)) * u[:, None]).astype(np.float32),
        "gi": (np.random.uniform(0.5, 1.5, (S, 1)) / u[:, None]).astype(np.float32),
        "offs": striped(np.random.permutation(T)[:S]),
        "two": striped(np.random.permutation(T)[:S]),
        "n1": striped8(np.random.randint(0, J, (8, H))),
        "n2": striped8(np.random.randint(0, J, (8, H))),
        "n3": striped8(np.stack([np.random.permutation(H) for _ in range(8)])),
        "n4": striped8(np.stack([np.random.permutation(N) for _ in range(8)])),
        "n5": striped8(np.stack([np.random.permutation(N) for _ in range(8)])),
    }


def reference(x_words, x_scales, wa, wb, tab, gt, gi, offs, two, n1, n2, n3, n4, n5):
    xq = unpack_weight(x_words, x_scales)[:, unstriped(offs)]
    a = xq.T @ mxq(f64(wa), 0, "e4m3")
    z = f64(gt) * ((a[np.arange(S)[:, None], runs(n3, S)]) * (f64(tab)[np.arange(S)[:, None], runs(n1, S)]) + f64(tab)[np.arange(S)[:, None], runs(n2, S)])
    x_two = unpack_weight(x_words, x_scales)[:, unstriped(two)]
    b = x_two.T @ mxq(f64(wb), 0, "e4m3")
    z2 = f64(gi) * b
    cv = 0.0625 * ((mxq(z, 0, "e4m3").T @ mxq(z2, 0, "e4m3")))
    st = np.maximum(cv, cv[np.arange(H)[:, None], runs(n4, H)])
    return st[np.arange(H)[:, None], runs(n5, H)] - (0.5 * cv)

@@ -1,0 +1,240 @@
+from contextlib import ExitStack
+
+import concourse.mybir as mybir
+
+K, T, S, H, N = 512, 2048, 512, 512, 512
+FLOPS = 2 * K * S * H + 2 * K * S * N + 2 * S * H * N
+
+F32 = mybir.dt.float32
+BF16 = mybir.dt.bfloat16
+I32 = mybir.dt.int32
+U32 = mybir.dt.uint32
+U16 = mybir.dt.uint16
+U8 = mybir.dt.uint8
+FP8X4 = mybir.dt.float8_e4m3fn_x4
+COPY = mybir.ActivationFunctionType.Copy
+MULT = mybir.AluOpType.mult
+ADD = mybir.AluOpType.add
+SUB = mybir.AluOpType.subtract
+MAX = mybir.AluOpType.max
+
+P = 128
+PACK = 4
+W = 512
+HALF = W // 2
+
+
+def tile_picked_momkindahopb_none_p_kernel(
+    tc, x_words, x_scales, wa, wb, tab, gt, gi, offs, two, n1, n2, n3, n4, n5, out
+):
+    nc = tc.nc
+    with ExitStack() as ctx:
+        lists = ctx.enter_context(tc.tile_pool(name="lists", bufs=1))
+        sb = ctx.enter_context(tc.tile_pool(name="sb", bufs=1))
+        psum = ctx.enter_context(tc.psum_pool(name="psum", bufs=1))
+
+        def load_list(name, src):
+            tile = lists.tile([P, W // 16], U16, name=name)
+            nc.sync.dma_start(tile[:], src)
+            return tile
+
+        def cols(h):
+            return slice(h * HALF, (h + 1) * HALF)
+
+        def entries(tile, h):
+            return tile[:, h * HALF // 16 : (h + 1) * HALF // 16]
+
+        tab_rows = tab.rearrange("(p t) j -> t p j", t=PACK)
+        out_rows = out.rearrange("(p t) j -> t p j", t=PACK)
+
+        def load_tab(t):
+            tile = sb.tile([P, W], F32, name="tab%d" % t)
+            nc.sync.dma_start(tile[:], tab_rows[t])
+            return tile
+
+        def load_weight(name, src, h):
+            tile = sb.tile([P, PACK, HALF], F32, name="%s_raw%d" % (name, h))
+            nc.sync.dma_start(tile[:], src.rearrange("(p t) c -> p t c", t=PACK)[:, :, cols(h)])
+            return tile
+
+        def load_gain(name, src):
+            tile = sb.tile([P, PACK], F32, name=name)
+            nc.sync.dma_start(tile[:], src.rearrange("(p t) o -> p (t o)", t=PACK))
+            return tile
+
+        xs = sb.tile([P, T], U8, name="xs", align_bytes=64)
+        nc.vector.memset(xs[:].bitcast(I32), 0)
+        for q in range(4):
+            nc.gpsimd.dma_start(
+                xs[32 * q : 32 * q + 4, :].bitcast(I32), x_scales[0, 4 * q : 4 * q + 4, :].bitcast(I32)
+            )
+
+        n1_sb = load_list("n1", n1)
+        tab_sb = [load_tab(0), load_tab(1)]
+        xw = sb.tile([P, T], I32, name="xw", align_bytes=64)
+        nc.sync.dma_start(xw[:], x_words[0].rearrange("p n t -> p (n t)").bitcast(I32))
+        tab_sb.extend([load_tab(2), load_tab(3)])
+        offs_sb = load_list("offs", offs)
+        wa_raw = [load_weight("wa", wa, h) for h in range(2)]
+        two_sb = load_list("two", two)
+        wb_raw = [load_weight("wb", wb, h) for h in range(2)]
+        gt_sb = load_gain("gt", gt)
+        n3_sb = load_list("n3", n3)
+        n2_sb = load_list("n2", n2)
+        gi_sb = load_gain("gi", gi)
+        n4_sb = load_list("n4", n4)
+        n5_sb = load_list("n5", n5)
+
+        warm = sb.tile([P, 1], F32, name="warm")
+        nc.vector.memset(warm[:], 0.0)
+        warm_out = sb.tile([P, 1], F32, name="warm_out")
+        nc.scalar.activation(warm_out[:], warm[:], COPY)
+
+        def gather_t1(t):
+            tile = sb.tile([P, W], F32, name="t1_%d" % t)
+            for h in range(2):
+                nc.vector.tensor_copy(tile[:, cols(h)], tab_sb[t][:].indirect(entries(n1_sb, h)))
+            return tile
+
+        def pick(name, lst):
+            words = sb.tile([P, S], U32, name=name + "_w", align_bytes=64)
+            scales = sb.tile([P, S], U8, name=name + "_s", align_bytes=64)
+            nc.vector.tensor_copy(words[:], xw[:].bitcast(U32).indirect(lst[:]))
+            nc.vector.tensor_copy(scales[:], xs[:].indirect(lst[:]))
+            dwords = sb.tile([P, S], U32, name=name + "_dw", align_bytes=64)
+            dscales = sb.tile([P, S], U8, name=name + "_ds", align_bytes=64)
+            nc.vector.tensor_copy(
+                dwords[:].rearrange("p (t b i) -> p b t i", t=PACK, i=4),
+                words[:].rearrange("p (b i t) -> p b t i", t=PACK, i=4),
+            )
+            nc.vector.tensor_copy(
+                dscales[:].rearrange("p (t b i) -> p b t i", t=PACK, i=16),
+                scales[:].rearrange("p (b i t) -> p b t i", t=PACK, i=16),
+            )
+            return dwords, dscales
+
+        def interleave(grouped, planes):
+            nc.scalar.copy(
+                grouped.rearrange("p (c i t) -> p c t i", t=PACK, i=4),
+                planes.rearrange("p t (c i) -> p c t i", i=4),
+            )
+
+        def quantize(name, grouped, width):
+            codes = sb.tile([P, width], U32, name=name + "_q", align_bytes=64)
+            scales = sb.tile([P, width], U8, name=name + "_qs", align_bytes=64)
+            nc.vector.quantize_mx(out=codes[:].bitcast(FP8X4), scales=scales[:], in_=grouped)
+            return codes, scales
+
+        def weight_planes(name, raw):
+            grouped = sb.tile([P, PACK * W], BF16, name=name + "_g", align_bytes=64)
+            for h in range(2):
+                interleave(grouped[:, h * PACK * HALF : (h + 1) * PACK * HALF], raw[h][:])
+            return grouped
+
+        def product(bank, lhs, lhs_cols, rhs):
+            acc = psum.tile([P, W], F32, name="acc", tag="bank%d" % bank)
+            nc.tensor.matmul_mx(
+                out=acc[:],
+                lhsT=lhs[0][:, lhs_cols].bitcast(FP8X4),
+                lhsT_scale=lhs[1][:, lhs_cols],
+                rhs=rhs[0][:].bitcast(FP8X4),
+                rhs_scale=rhs[1][:],
+                start=True,
+                stop=True,
+            )
+            return acc
+
+        t1 = [gather_t1(0), gather_t1(1)]
+        tabg = []
+        for t in range(PACK):
+            tile = sb.tile([P, W], F32, name="tabg%d" % t)
+            nc.scalar.activation(tile[:], tab_sb[t][:], COPY, scale=gt_sb[:, t : t + 1])
+            tabg.append(tile)
+        wa_g = weight_planes("wa", wa_raw)
+        xa = pick("xa", offs_sb)
+        t1.append(gather_t1(2))
+        wa_q = quantize("wa", wa_g[:], W)
+        ag = []
+        for t in range(PACK):
+            acc = product(t, xa, slice(t * P, (t + 1) * P), wa_q)
+            tile = sb.tile([P, W], F32, name="ag%d" % t)
+            nc.scalar.activation(tile[:], acc[:], COPY, scale=gt_sb[:, t : t + 1])
+            ag.append(tile)
+        wb_g = weight_planes("wb", wb_raw)
+        xb = pick("xb", two_sb)
+        t1.append(gather_t1(3))
+
+        prod = sb.tile([P, PACK, W], F32, name="prod")
+        z = [sb.tile([P, PACK, HALF], F32, name="z%d" % h) for h in range(2)]
+        z_g = sb.tile([P, PACK, P, PACK], BF16, name="z_g", align_bytes=64)
+
+        def make_prod(h):
+            for t in range(PACK):
+                nc.vector.tensor_tensor(
+                    prod[:, t, cols(h)], ag[t][:].indirect(entries(n3_sb, h)), t1[t][:, cols(h)], MULT
+                )
+
+        def make_z(h):
+            for t in range(PACK):
+                nc.vector.tensor_tensor(
+                    z[h][:, t, :], tabg[t][:].indirect(entries(n2_sb, h)), prod[:, t, cols(h)], ADD
+                )
+
+        def z_views(h):
+            m = HALF // PACK
+            return (
+                z_g[:, :, h * m : (h + 1) * m, :].rearrange("p u m t -> p m t u"),
+                z[h][:].rearrange("p t (m u) -> p m t u", u=PACK),
+            )
+
+        make_prod(0)
+        wb_q = quantize("wb", wb_g[:], W)
+        z2p = sb.tile([P, PACK, W], BF16, name="z2p")
+        for t in range(PACK):
+            acc = product(PACK + t, xb, slice(t * P, (t + 1) * P), wb_q)
+            nc.scalar.activation(z2p[:, t, :], acc[:], COPY, scale=gi_sb[:, t : t + 1])
+        z2_g = sb.tile([P, PACK * W], BF16, name="z2_g", align_bytes=64)
+        interleave(z2_g[:], z2p[:])
+        make_z(0)
+        nc.scalar.copy(*z_views(0))
+        make_prod(1)
+        z2_q = quantize("z2", z2_g[:], W)
+        make_z(1)
+        nc.vector.tensor_copy(*z_views(1))
+
+        cv, half_cv = [], []
+        for u in range(PACK):
+            z_q = quantize("zrow%d" % u, z_g[:, u].rearrange("p m t -> p (m t)"), P)
+            acc = product(u, z_q, slice(0, P), z2_q)
+            whole = sb.tile([P, W], F32, name="cv%d" % u)
+            nc.scalar.activation(whole[:], acc[:], COPY, scale=0.0625)
+            cv.append(whole)
+            half_cv.append((acc, sb.tile([P, W], F32, name="hcv%d" % u)))
+        for acc, tile in half_cv:
+            nc.scalar.activation(tile[:], acc[:], COPY, scale=0.03125)
+
+        g4 = [sb.tile([P, W], F32, name="g4_%d" % u) for u in range(PACK)]
+        st = [sb.tile([P, W], F32, name="st%d" % u) for u in range(PACK)]
+        res = [sb.tile([P, W], F32, name="res%d" % u) for u in range(PACK)]
+
+        def hop(u):
+            for h in range(2):
+                nc.vector.tensor_copy(g4[u][:, cols(h)], cv[u][:].indirect(entries(n4_sb, h)))
+
+        def larger(u):
+            nc.vector.tensor_tensor(st[u][:], g4[u][:], cv[u][:], MAX)
+
+        def finish(u):
+            for h in range(2):
+                nc.vector.tensor_tensor(
+                    res[u][:, cols(h)], st[u][:].indirect(entries(n5_sb, h)), half_cv[u][1][:, cols(h)], SUB
+                )
+            nc.sync.dma_start(out_rows[u], res[u][:])
+
+        for step in range(PACK + 2):
+            if step < PACK:
+                hop(step)
+            if 1 <= step <= PACK:
+                larger(step - 1)
+            if step >= 2:
+                finish(step - 2)

@@ -44,13 +44,21 @@ def tile_picked_momkindahopb_none_p_kernel(
         def entries(tile, h):
             return tile[:, h * HALF // 16 : (h + 1) * HALF // 16]
 
+        def wide_tiles(name):
+            return [sb.tile([P, 2 * W], F32, name="%s%d" % (name, t)) for t in range(PACK)]
+
         tab_rows = tab.rearrange("(p t) j -> t p j", t=PACK)
         out_rows = out.rearrange("(p t) j -> t p j", t=PACK)
+        tab_w = wide_tiles("tab_w")
+        a_w = wide_tiles("a_w")
+        cv_w = wide_tiles("cv_w")
+        st_w = wide_tiles("st_w")
+        t1 = [a_w[(t - 1) % PACK][:, W:] for t in range(PACK)]
+        prod = [cv_w[t][:, W:] for t in range(PACK)]
+        hopped = [st_w[t][:, W:] for t in range(PACK)]
 
         def load_tab(t):
-            tile = sb.tile([P, W], F32, name="tab%d" % t)
-            nc.sync.dma_start(tile[:], tab_rows[t])
-            return tile
+            nc.sync.dma_start(tab_w[t][:, :W], tab_rows[t])
 
         def load_weight(name, src, h):
             tile = sb.tile([P, PACK, HALF], F32, name="%s_raw%d" % (name, h))
@@ -59,59 +67,57 @@ def tile_picked_momkindahopb_none_p_kernel(
 
         def load_gain(name, src):
             tile = sb.tile([P, PACK], F32, name=name)
-            nc.sync.dma_start(tile[:], src.rearrange("(p t) o -> p (t o)", t=PACK))
+            nc.gpsimd.dma_start(tile[:], src.rearrange("(p t) o -> p (t o)", t=PACK))
             return tile
 
         xs = sb.tile([P, T], U8, name="xs", align_bytes=64)
         nc.vector.memset(xs[:].bitcast(I32), 0)
-        for q in range(4):
-            nc.gpsimd.dma_start(
-                xs[32 * q : 32 * q + 4, :].bitcast(I32), x_scales[0, 4 * q : 4 * q + 4, :].bitcast(I32)
-            )
+        nc.vector.memset(tab_w[0][:, W:], 0.0)
+        nc.vector.memset(tab_w[1][:, W:], 0.0)
+        nc.gpsimd.memset(tab_w[2][:, W:], 0.0)
+        gt_sb = load_gain("gt", gt)
+        nc.gpsimd.memset(tab_w[3][:, W:], 0.0)
+        gi_sb = load_gain("gi", gi)
 
+        load_tab(0)
         n1_sb = load_list("n1", n1)
-        tab_sb = [load_tab(0), load_tab(1)]
+        load_tab(1)
+        load_tab(2)
         xw = sb.tile([P, T], I32, name="xw", align_bytes=64)
         nc.sync.dma_start(xw[:], x_words[0].rearrange("p n t -> p (n t)").bitcast(I32))
-        tab_sb.extend([load_tab(2), load_tab(3)])
+        for q in range(4):
+            nc.scalar.dma_start(
+                xs[32 * q : 32 * q + 4, :].bitcast(I32), x_scales[0, 4 * q : 4 * q + 4, :].bitcast(I32)
+            )
         offs_sb = load_list("offs", offs)
         wa_raw = [load_weight("wa", wa, h) for h in range(2)]
         two_sb = load_list("two", two)
         wb_raw = [load_weight("wb", wb, h) for h in range(2)]
-        gt_sb = load_gain("gt", gt)
+        load_tab(3)
         n3_sb = load_list("n3", n3)
         n2_sb = load_list("n2", n2)
-        gi_sb = load_gain("gi", gi)
         n4_sb = load_list("n4", n4)
         n5_sb = load_list("n5", n5)
 
-        warm = sb.tile([P, 1], F32, name="warm")
-        nc.vector.memset(warm[:], 0.0)
-        warm_out = sb.tile([P, 1], F32, name="warm_out")
-        nc.scalar.activation(warm_out[:], warm[:], COPY)
-
         def gather_t1(t):
-            tile = sb.tile([P, W], F32, name="t1_%d" % t)
-            for h in range(2):
-                nc.vector.tensor_copy(tile[:, cols(h)], tab_sb[t][:].indirect(entries(n1_sb, h)))
-            return tile
+            nc.vector.tensor_copy(t1[t], tab_w[t][:].indirect(n1_sb[:]))
 
         def pick(name, lst):
-            words = sb.tile([P, S], U32, name=name + "_w", align_bytes=64)
-            scales = sb.tile([P, S], U8, name=name + "_s", align_bytes=64)
-            nc.vector.tensor_copy(words[:], xw[:].bitcast(U32).indirect(lst[:]))
-            nc.vector.tensor_copy(scales[:], xs[:].indirect(lst[:]))
             dwords = sb.tile([P, S], U32, name=name + "_dw", align_bytes=64)
-            dscales = sb.tile([P, S], U8, name=name + "_ds", align_bytes=64)
             nc.vector.tensor_copy(
-                dwords[:].rearrange("p (t b i) -> p b t i", t=PACK, i=4),
-                words[:].rearrange("p (b i t) -> p b t i", t=PACK, i=4),
+                dwords[:].rearrange("p (t m) -> p m t", t=PACK), xw[:].bitcast(U32).indirect(lst[:])
             )
+            return dwords
+
+        def pick_scales(name, lst):
+            scales = sb.tile([P, S], U8, name=name + "_s", align_bytes=64)
+            nc.vector.tensor_copy(scales[:], xs[:].indirect(lst[:]))
+            dscales = sb.tile([P, S], U8, name=name + "_ds", align_bytes=64)
             nc.vector.tensor_copy(
                 dscales[:].rearrange("p (t b i) -> p b t i", t=PACK, i=16),
                 scales[:].rearrange("p (b i t) -> p b t i", t=PACK, i=16),
             )
-            return dwords, dscales
+            return dscales
 
         def interleave(grouped, planes):
             nc.scalar.copy(
@@ -131,105 +137,104 @@ def tile_picked_momkindahopb_none_p_kernel(
                 interleave(grouped[:, h * PACK * HALF : (h + 1) * PACK * HALF], raw[h][:])
             return grouped
 
-        def product(bank, lhs, lhs_cols, rhs):
-            acc = psum.tile([P, W], F32, name="acc", tag="bank%d" % bank)
+        def product(bank, lhs, lhs_cols, rhs, rhs_cols=slice(0, W)):
+            acc = psum.tile([P, rhs_cols.stop - rhs_cols.start], F32, name="acc", tag="bank%d" % bank)
             nc.tensor.matmul_mx(
                 out=acc[:],
                 lhsT=lhs[0][:, lhs_cols].bitcast(FP8X4),
                 lhsT_scale=lhs[1][:, lhs_cols],
-                rhs=rhs[0][:].bitcast(FP8X4),
-                rhs_scale=rhs[1][:],
+                rhs=rhs[0][:, rhs_cols].bitcast(FP8X4),
+                rhs_scale=rhs[1][:, rhs_cols],
                 start=True,
                 stop=True,
             )
             return acc
 
-        t1 = [gather_t1(0), gather_t1(1)]
-        tabg = []
-        for t in range(PACK):
-            tile = sb.tile([P, W], F32, name="tabg%d" % t)
-            nc.scalar.activation(tile[:], tab_sb[t][:], COPY, scale=gt_sb[:, t : t + 1])
-            tabg.append(tile)
+        tabg = [sb.tile([P, W], F32, name="tabg%d" % t) for t in range(PACK)]
+
+        def scale_tab(t):
+            nc.scalar.activation(tabg[t][:], tab_w[t][:, :W], COPY, scale=gt_sb[:, t : t + 1])
+
+        for t in range(PACK - 1):
+            gather_t1(t)
+            scale_tab(t)
         wa_g = weight_planes("wa", wa_raw)
-        xa = pick("xa", offs_sb)
-        t1.append(gather_t1(2))
+        xa = pick("xa", offs_sb), pick_scales("xa", offs_sb)
+        xb_words = pick("xb", two_sb)
         wa_q = quantize("wa", wa_g[:], W)
-        ag = []
+        xb = xb_words, pick_scales("xb", two_sb)
+        wb_g = weight_planes("wb", wb_raw)
+        gather_t1(3)
         for t in range(PACK):
             acc = product(t, xa, slice(t * P, (t + 1) * P), wa_q)
-            tile = sb.tile([P, W], F32, name="ag%d" % t)
-            nc.scalar.activation(tile[:], acc[:], COPY, scale=gt_sb[:, t : t + 1])
-            ag.append(tile)
-        wb_g = weight_planes("wb", wb_raw)
-        xb = pick("xb", two_sb)
-        t1.append(gather_t1(3))
-
-        prod = sb.tile([P, PACK, W], F32, name="prod")
-        z = [sb.tile([P, PACK, HALF], F32, name="z%d" % h) for h in range(2)]
-        z_g = sb.tile([P, PACK, P, PACK], BF16, name="z_g", align_bytes=64)
-
-        def make_prod(h):
-            for t in range(PACK):
-                nc.vector.tensor_tensor(
-                    prod[:, t, cols(h)], ag[t][:].indirect(entries(n3_sb, h)), t1[t][:, cols(h)], MULT
-                )
-
-        def make_z(h):
-            for t in range(PACK):
-                nc.vector.tensor_tensor(
-                    z[h][:, t, :], tabg[t][:].indirect(entries(n2_sb, h)), prod[:, t, cols(h)], ADD
-                )
-
-        def z_views(h):
-            m = HALF // PACK
-            return (
-                z_g[:, :, h * m : (h + 1) * m, :].rearrange("p u m t -> p m t u"),
-                z[h][:].rearrange("p t (m u) -> p m t u", u=PACK),
-            )
-
-        make_prod(0)
+            nc.scalar.activation(a_w[t][:, :W], acc[:], COPY, scale=gt_sb[:, t : t + 1])
         wb_q = quantize("wb", wb_g[:], W)
+        scale_tab(3)
         z2p = sb.tile([P, PACK, W], BF16, name="z2p")
         for t in range(PACK):
             acc = product(PACK + t, xb, slice(t * P, (t + 1) * P), wb_q)
             nc.scalar.activation(z2p[:, t, :], acc[:], COPY, scale=gi_sb[:, t : t + 1])
         z2_g = sb.tile([P, PACK * W], BF16, name="z2_g", align_bytes=64)
         interleave(z2_g[:], z2p[:])
+
+        for t in range(PACK):
+            nc.vector.tensor_tensor(prod[t], a_w[t][:].indirect(n3_sb[:]), t1[t], MULT)
+
+        z = [sb.tile([P, PACK, HALF], F32, name="z%d" % h) for h in range(2)]
+        zg_first = sb.tile([P, 1, P, PACK], BF16, name="zg_first", align_bytes=64)
+        zg_rest = sb.tile([P, PACK - 1, P, PACK], BF16, name="zg_rest", align_bytes=64)
+
+        def make_z(h):
+            for t in range(PACK):
+                nc.vector.tensor_tensor(
+                    z[h][:, t, :], tabg[t][:].indirect(entries(n2_sb, h)), prod[t][:, cols(h)], ADD
+                )
+
+        def z_views(h):
+            m = slice(h * HALF // PACK, (h + 1) * HALF // PACK)
+            src = z[h][:].rearrange("p t (m u) -> p m t u", u=PACK)
+            return (
+                (zg_first[:, :, m, :].rearrange("p u m t -> p m t u"), src[:, :, :, 0:1]),
+                (zg_rest[:, :, m, :].rearrange("p u m t -> p m t u"), src[:, :, :, 1:PACK]),
+            )
+
         make_z(0)
-        nc.scalar.copy(*z_views(0))
-        make_prod(1)
+        for dst, src in z_views(0):
+            nc.scalar.copy(dst, src)
         z2_q = quantize("z2", z2_g[:], W)
         make_z(1)
-        nc.vector.tensor_copy(*z_views(1))
-
-        cv, half_cv = [], []
+        half_cv = [sb.tile([P, W], F32, name="hcv%d" % u) for u in range(PACK)]
+        accs = []
         for u in range(PACK):
-            z_q = quantize("zrow%d" % u, z_g[:, u].rearrange("p m t -> p (m t)"), P)
-            acc = product(u, z_q, slice(0, P), z2_q)
-            whole = sb.tile([P, W], F32, name="cv%d" % u)
-            nc.scalar.activation(whole[:], acc[:], COPY, scale=0.0625)
-            cv.append(whole)
-            half_cv.append((acc, sb.tile([P, W], F32, name="hcv%d" % u)))
-        for acc, tile in half_cv:
-            nc.scalar.activation(tile[:], acc[:], COPY, scale=0.03125)
+            if u < 2:
+                nc.vector.tensor_copy(*z_views(1)[u])
+            grouped = zg_first[:, 0] if u == 0 else zg_rest[:, u - 1]
+            z_q = quantize("zrow%d" % u, grouped.rearrange("p m t -> p (m t)"), P)
+            for c in [cols(0), cols(1)] if u == 0 else [slice(0, W)]:
+                acc = product(len(accs), z_q, slice(0, P), z2_q, c)
+                nc.scalar.activation(cv_w[u][:, c], acc[:], COPY, scale=0.0625)
+                accs.append((acc, half_cv[u][:, c]))
+        for acc, dst in accs:
+            nc.scalar.activation(dst, acc[:], COPY, scale=0.03125)
 
-        g4 = [sb.tile([P, W], F32, name="g4_%d" % u) for u in range(PACK)]
-        st = [sb.tile([P, W], F32, name="st%d" % u) for u in range(PACK)]
         res = [sb.tile([P, W], F32, name="res%d" % u) for u in range(PACK)]
 
         def hop(u):
-            for h in range(2):
-                nc.vector.tensor_copy(g4[u][:, cols(h)], cv[u][:].indirect(entries(n4_sb, h)))
+            nc.vector.tensor_copy(hopped[u], cv_w[u][:].indirect(n4_sb[:]))
 
         def larger(u):
-            nc.vector.tensor_tensor(st[u][:], g4[u][:], cv[u][:], MAX)
+            nc.vector.tensor_tensor(st_w[u][:, :W], hopped[u], cv_w[u][:, :W], MAX)
 
         def finish(u):
-            for h in range(2):
-                nc.vector.tensor_tensor(
-                    res[u][:, cols(h)], st[u][:].indirect(entries(n5_sb, h)), half_cv[u][1][:, cols(h)], SUB
-                )
-            nc.sync.dma_start(out_rows[u], res[u][:])
+            if u < PACK - 1:
+                nc.vector.tensor_tensor(res[u][:], st_w[u][:].indirect(n5_sb[:]), half_cv[u][:], SUB)
+                nc.sync.dma_start(out_rows[u], res[u][:])
+            else:
+                for h in range(2):
+                    nc.vector.tensor_tensor(
+                        res[u][:, cols(h)], st_w[u][:].indirect(entries(n5_sb, h)), half_cv[u][:, cols(h)], SUB
+                    )
+                    nc.sync.dma_start(out_rows[u][:, cols(h)], res[u][:, cols(h)])
 
         for step in range(PACK + 2):
             if step < PACK:

@@ -1,6 +1,7 @@
 from contextlib import ExitStack
 
 import concourse.mybir as mybir
+from concourse.masks import make_identity
 
 K, T, S, H, N = 512, 2048, 512, 512, 512
 FLOPS = 2 * K * S * H + 2 * K * S * N + 2 * S * H * N
@@ -12,6 +13,7 @@ U32 = mybir.dt.uint32
 U16 = mybir.dt.uint16
 U8 = mybir.dt.uint8
 FP8X4 = mybir.dt.float8_e4m3fn_x4
+RELU = mybir.ActivationFunctionType.Relu
 COPY = mybir.ActivationFunctionType.Copy
 MULT = mybir.AluOpType.mult
 ADD = mybir.AluOpType.add
@@ -22,6 +24,7 @@ P = 128
 PACK = 4
 W = 512
 HALF = W // 2
+TURNED = (1, 2)
 
 
 def tile_picked_momkindahopb_none_p_kernel(
@@ -78,6 +81,10 @@ def tile_picked_momkindahopb_none_p_kernel(
         gt_sb = load_gain("gt", gt)
         nc.gpsimd.memset(tab_w[3][:, W:], 0.0)
         gi_sb = load_gain("gi", gi)
+        ident = sb.tile([P, P], F32, name="ident")
+        make_identity(nc, ident[:])
+        for u in TURNED:
+            nc.gpsimd.memset(st_w[u][:, W:], 0.0)
 
         load_tab(0)
         n1_sb = load_list("n1", n1)
@@ -109,8 +116,8 @@ def tile_picked_momkindahopb_none_p_kernel(
             )
             return dwords
 
-        def pick_scales(name, lst):
-            scales = sb.tile([P, S], U8, name=name + "_s", align_bytes=64)
+        def pick_scales(name, lst, tag):
+            scales = sb.tile([P, S], U8, name=name + "_s", tag=tag, align_bytes=64)
             nc.vector.tensor_copy(scales[:], xs[:].indirect(lst[:]))
             dscales = sb.tile([P, S], U8, name=name + "_ds", align_bytes=64)
             nc.vector.tensor_copy(
@@ -159,10 +166,10 @@ def tile_picked_momkindahopb_none_p_kernel(
             gather_t1(t)
             scale_tab(t)
         wa_g = weight_planes("wa", wa_raw)
-        xa = pick("xa", offs_sb), pick_scales("xa", offs_sb)
+        xa = pick("xa", offs_sb), pick_scales("xa", offs_sb, "xa_s")
         xb_words = pick("xb", two_sb)
         wa_q = quantize("wa", wa_g[:], W)
-        xb = xb_words, pick_scales("xb", two_sb)
+        xb = xb_words, pick_scales("xb", two_sb, "wa_g")
         wb_g = weight_planes("wb", wb_raw)
         gather_t1(3)
         for t in range(PACK):
@@ -170,21 +177,22 @@ def tile_picked_momkindahopb_none_p_kernel(
             nc.scalar.activation(a_w[t][:, :W], acc[:], COPY, scale=gt_sb[:, t : t + 1])
         wb_q = quantize("wb", wb_g[:], W)
         scale_tab(3)
-        z2p = sb.tile([P, PACK, W], BF16, name="z2p")
+        z2p = sb.tile([P, PACK, W], BF16, name="z2p", align_bytes=64)
         for t in range(PACK):
             acc = product(PACK + t, xb, slice(t * P, (t + 1) * P), wb_q)
             nc.scalar.activation(z2p[:, t, :], acc[:], COPY, scale=gi_sb[:, t : t + 1])
-        z2_g = sb.tile([P, PACK * W], BF16, name="z2_g", align_bytes=64)
-        interleave(z2_g[:], z2p[:])
+        z2_g = [sb.tile([P, PACK * HALF], BF16, name="z2_g%d" % h, align_bytes=64) for h in range(2)]
+        for h in range(2):
+            interleave(z2_g[h][:], z2p[:, :, cols(h)])
 
         for t in range(PACK):
             nc.vector.tensor_tensor(prod[t], a_w[t][:].indirect(n3_sb[:]), t1[t], MULT)
 
-        z = [sb.tile([P, PACK, HALF], F32, name="z%d" % h) for h in range(2)]
-        zg_first = sb.tile([P, 1, P, PACK], BF16, name="zg_first", align_bytes=64)
-        zg_rest = sb.tile([P, PACK - 1, P, PACK], BF16, name="zg_rest", align_bytes=64)
 
-        def make_z(h):
+        z = []
+
+        def make_z(h, tag):
+            z.append(sb.tile([P, PACK, HALF], F32, name="z%d" % h, tag=tag, align_bytes=64))
             for t in range(PACK):
                 nc.vector.tensor_tensor(
                     z[h][:, t, :], tabg[t][:].indirect(entries(n2_sb, h)), prod[t][:, cols(h)], ADD
@@ -198,36 +206,65 @@ def tile_picked_momkindahopb_none_p_kernel(
                 (zg_rest[:, :, m, :].rearrange("p u m t -> p m t u"), src[:, :, :, 1:PACK]),
             )
 
-        make_z(0)
+        make_z(0, "z0")
+        z2_q = (
+            sb.tile([P, W], U32, name="z2_q", align_bytes=64),
+            sb.tile([P, W], U8, name="z2_qs", align_bytes=64),
+        )
+        for h in range(2):
+            nc.vector.quantize_mx(
+                out=z2_q[0][:, cols(h)].bitcast(FP8X4), scales=z2_q[1][:, cols(h)], in_=z2_g[h][:]
+            )
+        zg_first = sb.tile([P, 1, P, PACK], BF16, name="zg_first", tag="z2p", align_bytes=64)
+        zg_rest = sb.tile([P, PACK - 1, P, PACK], BF16, name="zg_rest", tag="z2_g0", align_bytes=64)
         for dst, src in z_views(0):
             nc.scalar.copy(dst, src)
-        z2_q = quantize("z2", z2_g[:], W)
-        make_z(1)
-        half_cv = [sb.tile([P, W], F32, name="hcv%d" % u) for u in range(PACK)]
+        make_z(1, "z2_g1")
+        half_copy = {u: sb.tile([P, W], F32, name="hcv%d" % u) for u in TURNED}
+        half_cv = [half_copy[u][:] if u in TURNED else cv_w[u][:, :W] for u in range(PACK)]
         accs = []
+        banks = 0
         for u in range(PACK):
-            if u < 2:
-                nc.vector.tensor_copy(*z_views(1)[u])
             grouped = zg_first[:, 0] if u == 0 else zg_rest[:, u - 1]
+            nc.vector.tensor_copy(
+                grouped[:, P // 2 :, :], z[1][:].rearrange("p t (m u) -> p u m t", u=PACK)[:, u]
+            )
             z_q = quantize("zrow%d" % u, grouped.rearrange("p m t -> p (m t)"), P)
+            accs.append([])
             for c in [cols(0), cols(1)] if u == 0 else [slice(0, W)]:
-                acc = product(len(accs), z_q, slice(0, P), z2_q, c)
-                nc.scalar.activation(cv_w[u][:, c], acc[:], COPY, scale=0.0625)
-                accs.append((acc, half_cv[u][:, c]))
-        for acc, dst in accs:
-            nc.scalar.activation(dst, acc[:], COPY, scale=0.03125)
+                acc = product(banks, z_q, slice(0, P), z2_q, c)
+                banks = banks + 1
+                nc.scalar.activation(cv_w[u][:, c], acc[:], COPY, scale=0.03125)
+                accs[u].append((acc, c))
+            if u in TURNED:
+                nc.scalar.activation(half_cv[u], acc[:], COPY, scale=0.03125)
 
         res = [sb.tile([P, W], F32, name="res%d" % u) for u in range(PACK)]
+        diff = {u: sb.tile([P, W], F32, name="diff%d" % u) for u in TURNED}
+
+        def turn(bank, terms, dst, func, scale):
+            acc = psum.tile([P, W], F32, name="turned", tag="bank%d" % bank)
+            steps = [(src, c) for src in terms for c in range(W // P)]
+            for i, (src, c) in enumerate(steps):
+                block = slice(c * P, (c + 1) * P)
+                nc.tensor.matmul(
+                    acc[:, block], src[:, block], ident[:], is_transpose=True, start=i == 0, stop=i == len(steps) - 1
+                )
+            nc.scalar.activation(dst, acc[:], func, scale=scale)
 
         def hop(u):
-            nc.vector.tensor_copy(hopped[u], cv_w[u][:].indirect(n4_sb[:]))
+            if u in TURNED:
+                nc.vector.tensor_tensor(diff[u][:], cv_w[u][:].indirect(n4_sb[:]), half_cv[u], SUB)
+            else:
+                nc.vector.tensor_scalar(hopped[u], cv_w[u][:].indirect(n4_sb[:]), 2.0, 0.0, MULT, ADD)
 
         def larger(u):
-            nc.vector.tensor_tensor(st_w[u][:, :W], hopped[u], cv_w[u][:, :W], MAX)
+            for acc, c in accs[u]:
+                nc.vector.scalar_tensor_tensor(st_w[u][:, c], acc[:], 0.0625, hopped[u][:, c], MULT, MAX)
 
-        def finish(u):
-            if u < PACK - 1:
-                nc.vector.tensor_tensor(res[u][:], st_w[u][:].indirect(n5_sb[:]), half_cv[u][:], SUB)
+        def finish(u, pieces):
+            if pieces == 1:
+                nc.vector.tensor_tensor(res[u][:], st_w[u][:].indirect(n5_sb[:]), half_cv[u], SUB)
                 nc.sync.dma_start(out_rows[u], res[u][:])
             else:
                 for h in range(2):
@@ -236,10 +273,21 @@ def tile_picked_momkindahopb_none_p_kernel(
                     )
                     nc.sync.dma_start(out_rows[u][:, cols(h)], res[u][:, cols(h)])
 
-        for step in range(PACK + 2):
-            if step < PACK:
-                hop(step)
-            if 1 <= step <= PACK:
-                larger(step - 1)
-            if step >= 2:
-                finish(step - 2)
+        hop(0)
+        hop(1)
+        larger(0)
+        hop(2)
+        hop(3)
+        half_t = {u: sb.tile([P, W], F32, name="half_t%d" % u) for u in TURNED}
+        gain_t = {u: sb.tile([P, W], F32, name="gain_t%d" % u) for u in TURNED}
+        for u, bank in zip(TURNED, (5, 6)):
+            turn(bank, [half_cv[u]], half_t[u][:], COPY, 1.0)
+        for u, bank in zip(TURNED, (7, 2)):
+            turn(bank, [diff[u][:]], gain_t[u][:], RELU, 1.0)
+        for u, bank in zip(TURNED, (3, 5)):
+            turn(bank, [half_t[u][:], gain_t[u][:]], st_w[u][:, :W], COPY, 2.0)
+        finish(0, 1)
+        larger(3)
+        finish(3, 1)
+        finish(1, 1)
+        finish(2, 2)

@@ -13,8 +13,8 @@ U32 = mybir.dt.uint32
 U16 = mybir.dt.uint16
 U8 = mybir.dt.uint8
 FP8X4 = mybir.dt.float8_e4m3fn_x4
-RELU = mybir.ActivationFunctionType.Relu
 COPY = mybir.ActivationFunctionType.Copy
+RELU = mybir.ActivationFunctionType.Relu
 MULT = mybir.AluOpType.mult
 ADD = mybir.AluOpType.add
 SUB = mybir.AluOpType.subtract
@@ -24,7 +24,9 @@ P = 128
 PACK = 4
 W = 512
 HALF = W // 2
-TURNED = (1, 2)
+STRIPE = 16
+QUADRANT = 32
+TURNED = (0, 1)
 
 
 def tile_picked_momkindahopb_none_p_kernel(
@@ -36,42 +38,43 @@ def tile_picked_momkindahopb_none_p_kernel(
         sb = ctx.enter_context(tc.tile_pool(name="sb", bufs=1))
         psum = ctx.enter_context(tc.psum_pool(name="psum", bufs=1))
 
-        def load_list(name, src):
-            tile = lists.tile([P, W // 16], U16, name=name)
-            nc.sync.dma_start(tile[:], src)
-            return tile
-
         def cols(h):
             return slice(h * HALF, (h + 1) * HALF)
 
-        def entries(tile, h):
-            return tile[:, h * HALF // 16 : (h + 1) * HALF // 16]
+        def entries(list_tile, h):
+            return list_tile[:, h * HALF // STRIPE : (h + 1) * HALF // STRIPE]
 
-        def wide_tiles(name):
-            return [sb.tile([P, 2 * W], F32, name="%s%d" % (name, t)) for t in range(PACK)]
+        def wide_tiles(name, row_tiles):
+            return {t: sb.tile([P, 2 * W], F32, name="%s%d" % (name, t)) for t in row_tiles}
+
+        tab_w = wide_tiles("tab_w", range(PACK))
+        a_w = wide_tiles("a_w", (0, 1, 3))
+        cv_w = wide_tiles("cv_w", range(PACK))
+        st_w = wide_tiles("st_w", range(PACK))
+        tab_n1 = [a_w[(t - 1) % PACK][:, W:] for t in range(PACK - 1)]
+        prod = [cv_w[t][:, W:] for t in range(PACK)]
+        hopped = [st_w[u][:, W:] for u in range(PACK)]
 
         tab_rows = tab.rearrange("(p t) j -> t p j", t=PACK)
-        out_rows = out.rearrange("(p t) j -> t p j", t=PACK)
-        tab_w = wide_tiles("tab_w")
-        a_w = wide_tiles("a_w")
-        cv_w = wide_tiles("cv_w")
-        st_w = wide_tiles("st_w")
-        t1 = [a_w[(t - 1) % PACK][:, W:] for t in range(PACK)]
-        prod = [cv_w[t][:, W:] for t in range(PACK)]
-        hopped = [st_w[t][:, W:] for t in range(PACK)]
+        out_rows = out.rearrange("(p u) j -> u p j", u=PACK)
+
+        def load_list(name, src):
+            list_tile = lists.tile([P, W // STRIPE], U16, name=name)
+            nc.sync.dma_start(list_tile[:], src)
+            return list_tile
 
         def load_tab(t):
             nc.sync.dma_start(tab_w[t][:, :W], tab_rows[t])
 
         def load_weight(name, src, h):
-            tile = sb.tile([P, PACK, HALF], F32, name="%s_raw%d" % (name, h))
-            nc.sync.dma_start(tile[:], src.rearrange("(p t) c -> p t c", t=PACK)[:, :, cols(h)])
-            return tile
+            raw = sb.tile([P, PACK, HALF], F32, name="%s_raw%d" % (name, h))
+            nc.sync.dma_start(raw[:], src.rearrange("(p t) c -> p t c", t=PACK)[:, :, cols(h)])
+            return raw
 
         def load_gain(name, src):
-            tile = sb.tile([P, PACK], F32, name=name)
-            nc.gpsimd.dma_start(tile[:], src.rearrange("(p t) o -> p (t o)", t=PACK))
-            return tile
+            gain = sb.tile([P, PACK], F32, name=name)
+            nc.gpsimd.dma_start(gain[:], src.rearrange("(p t) o -> p (t o)", t=PACK))
+            return gain
 
         xs = sb.tile([P, T], U8, name="xs", align_bytes=64)
         nc.vector.memset(xs[:].bitcast(I32), 0)
@@ -83,8 +86,6 @@ def tile_picked_momkindahopb_none_p_kernel(
         gi_sb = load_gain("gi", gi)
         ident = sb.tile([P, P], F32, name="ident")
         make_identity(nc, ident[:])
-        for u in TURNED:
-            nc.gpsimd.memset(st_w[u][:, W:], 0.0)
 
         load_tab(0)
         n1_sb = load_list("n1", n1)
@@ -92,9 +93,9 @@ def tile_picked_momkindahopb_none_p_kernel(
         load_tab(2)
         xw = sb.tile([P, T], I32, name="xw", align_bytes=64)
         nc.sync.dma_start(xw[:], x_words[0].rearrange("p n t -> p (n t)").bitcast(I32))
-        for q in range(4):
+        for q in range(P // QUADRANT):
             nc.scalar.dma_start(
-                xs[32 * q : 32 * q + 4, :].bitcast(I32), x_scales[0, 4 * q : 4 * q + 4, :].bitcast(I32)
+                xs[QUADRANT * q : QUADRANT * q + 4, :].bitcast(I32), x_scales[0, 4 * q : 4 * q + 4, :].bitcast(I32)
             )
         offs_sb = load_list("offs", offs)
         wa_raw = [load_weight("wa", wa, h) for h in range(2)]
@@ -106,45 +107,49 @@ def tile_picked_momkindahopb_none_p_kernel(
         n4_sb = load_list("n4", n4)
         n5_sb = load_list("n5", n5)
 
-        def gather_t1(t):
-            nc.vector.tensor_copy(t1[t], tab_w[t][:].indirect(n1_sb[:]))
+        def gather_tab_n1(t):
+            nc.vector.tensor_copy(tab_n1[t], tab_w[t][:].indirect(n1_sb[:]))
 
-        def pick(name, lst):
-            dwords = sb.tile([P, S], U32, name=name + "_dw", align_bytes=64)
+        def pick_words(name, list_tile):
+            words = sb.tile([P, S], U32, name=name + "_words", align_bytes=64)
             nc.vector.tensor_copy(
-                dwords[:].rearrange("p (t m) -> p m t", t=PACK), xw[:].bitcast(U32).indirect(lst[:])
+                words[:].rearrange("p (t m) -> p m t", t=PACK), xw[:].bitcast(U32).indirect(list_tile[:])
             )
-            return dwords
+            return words
 
-        def pick_scales(name, lst, tag):
-            scales = sb.tile([P, S], U8, name=name + "_s", tag=tag, align_bytes=64)
-            nc.vector.tensor_copy(scales[:], xs[:].indirect(lst[:]))
-            dscales = sb.tile([P, S], U8, name=name + "_ds", align_bytes=64)
+        def pick_scales(name, list_tile, tag):
+            picked = sb.tile([P, S], U8, name=name + "_picked", tag=tag, align_bytes=64)
+            nc.vector.tensor_copy(picked[:], xs[:].indirect(list_tile[:]))
+            dealt = sb.tile([P, S], U8, name=name + "_dealt", align_bytes=64)
             nc.vector.tensor_copy(
-                dscales[:].rearrange("p (t b i) -> p b t i", t=PACK, i=16),
-                scales[:].rearrange("p (b i t) -> p b t i", t=PACK, i=16),
+                dealt[:].rearrange("p (t b i) -> p b t i", t=PACK, i=16),
+                picked[:].rearrange("p (b i t) -> p b t i", t=PACK, i=16),
             )
-            return dscales
+            return dealt
 
-        def interleave(grouped, planes):
+        def interleave(grouped, row_tiles):
             nc.scalar.copy(
                 grouped.rearrange("p (c i t) -> p c t i", t=PACK, i=4),
-                planes.rearrange("p t (c i) -> p c t i", i=4),
+                row_tiles.rearrange("p t (c i) -> p c t i", i=4),
             )
 
-        def quantize(name, grouped, width):
-            codes = sb.tile([P, width], U32, name=name + "_q", align_bytes=64)
-            scales = sb.tile([P, width], U8, name=name + "_qs", align_bytes=64)
-            nc.vector.quantize_mx(out=codes[:].bitcast(FP8X4), scales=scales[:], in_=grouped)
-            return codes, scales
-
-        def weight_planes(name, raw):
-            grouped = sb.tile([P, PACK * W], BF16, name=name + "_g", align_bytes=64)
+        def interleave_weight(name, raw):
+            grouped = sb.tile([P, PACK * W], BF16, name=name + "_grouped", align_bytes=64)
             for h in range(2):
                 interleave(grouped[:, h * PACK * HALF : (h + 1) * PACK * HALF], raw[h][:])
             return grouped
 
-        def product(bank, lhs, lhs_cols, rhs, rhs_cols=slice(0, W)):
+        def mx_tiles(name, width):
+            codes = sb.tile([P, width], U32, name=name + "_codes", align_bytes=64)
+            scales = sb.tile([P, width], U8, name=name + "_scales", align_bytes=64)
+            return codes, scales
+
+        def quantize(name, grouped, width):
+            codes, scales = mx_tiles(name, width)
+            nc.vector.quantize_mx(out=codes[:].bitcast(FP8X4), scales=scales[:], in_=grouped)
+            return codes, scales
+
+        def product(bank, lhs, lhs_cols, rhs, rhs_cols):
             acc = psum.tile([P, rhs_cols.stop - rhs_cols.start], F32, name="acc", tag="bank%d" % bank)
             nc.tensor.matmul_mx(
                 out=acc[:],
@@ -157,137 +162,135 @@ def tile_picked_momkindahopb_none_p_kernel(
             )
             return acc
 
-        tabg = [sb.tile([P, W], F32, name="tabg%d" % t) for t in range(PACK)]
+        whole = slice(0, W)
+        tab_gt = [sb.tile([P, W], F32, name="tab_gt%d" % t) for t in range(PACK)]
 
         def scale_tab(t):
-            nc.scalar.activation(tabg[t][:], tab_w[t][:, :W], COPY, scale=gt_sb[:, t : t + 1])
+            nc.scalar.activation(tab_gt[t][:], tab_w[t][:, :W], COPY, scale=gt_sb[:, t : t + 1])
 
         for t in range(PACK - 1):
-            gather_t1(t)
+            gather_tab_n1(t)
             scale_tab(t)
-        wa_g = weight_planes("wa", wa_raw)
-        xa = pick("xa", offs_sb), pick_scales("xa", offs_sb, "xa_s")
-        xb_words = pick("xb", two_sb)
-        wa_q = quantize("wa", wa_g[:], W)
-        xb = xb_words, pick_scales("xb", two_sb, "wa_g")
-        wb_g = weight_planes("wb", wb_raw)
-        gather_t1(3)
+        wa_grouped = interleave_weight("wa", wa_raw)
+        xa = pick_words("xa", offs_sb), pick_scales("xa", offs_sb, "xa_picked")
+        xb_words = pick_words("xb", two_sb)
+        wa_q = quantize("wa", wa_grouped[:], W)
+        xb = xb_words, pick_scales("xb", two_sb, "wa_grouped")
+        wb_grouped = interleave_weight("wb", wb_raw)
+        wb_q = quantize("wb", wb_grouped[:], W)
+        a_w[2] = sb.tile([P, 2 * W], F32, name="a_w2", tag="wb_grouped", align_bytes=64)
+        tab_n1.append(a_w[2][:, W:])
+        gather_tab_n1(3)
         for t in range(PACK):
-            acc = product(t, xa, slice(t * P, (t + 1) * P), wa_q)
+            acc = product(t, xa, slice(t * P, (t + 1) * P), wa_q, whole)
             nc.scalar.activation(a_w[t][:, :W], acc[:], COPY, scale=gt_sb[:, t : t + 1])
-        wb_q = quantize("wb", wb_g[:], W)
         scale_tab(3)
-        z2p = sb.tile([P, PACK, W], BF16, name="z2p", align_bytes=64)
+
+        z2_rows = sb.tile([P, PACK, W], BF16, name="z2_rows", align_bytes=64)
         for t in range(PACK):
-            acc = product(PACK + t, xb, slice(t * P, (t + 1) * P), wb_q)
-            nc.scalar.activation(z2p[:, t, :], acc[:], COPY, scale=gi_sb[:, t : t + 1])
-        z2_g = [sb.tile([P, PACK * HALF], BF16, name="z2_g%d" % h, align_bytes=64) for h in range(2)]
+            acc = product(PACK + t, xb, slice(t * P, (t + 1) * P), wb_q, whole)
+            nc.scalar.activation(z2_rows[:, t, :], acc[:], COPY, scale=gi_sb[:, t : t + 1])
+        z2_grouped = [sb.tile([P, PACK * HALF], BF16, name="z2_grouped%d" % h, align_bytes=64) for h in range(2)]
         for h in range(2):
-            interleave(z2_g[h][:], z2p[:, :, cols(h)])
+            interleave(z2_grouped[h][:], z2_rows[:, :, cols(h)])
 
         for t in range(PACK):
-            nc.vector.tensor_tensor(prod[t], a_w[t][:].indirect(n3_sb[:]), t1[t], MULT)
-
-
-        z = []
+            nc.vector.tensor_tensor(prod[t], a_w[t][:].indirect(n3_sb[:]), tab_n1[t], MULT)
 
         def make_z(h, tag):
-            z.append(sb.tile([P, PACK, HALF], F32, name="z%d" % h, tag=tag, align_bytes=64))
+            z_half = sb.tile([P, PACK, HALF], F32, name="z%d" % h, tag=tag, align_bytes=64)
             for t in range(PACK):
                 nc.vector.tensor_tensor(
-                    z[h][:, t, :], tabg[t][:].indirect(entries(n2_sb, h)), prod[t][:, cols(h)], ADD
+                    z_half[:, t, :], tab_gt[t][:].indirect(entries(n2_sb, h)), prod[t][:, cols(h)], ADD
                 )
+            return z_half
 
-        def z_views(h):
-            m = slice(h * HALF // PACK, (h + 1) * HALF // PACK)
-            src = z[h][:].rearrange("p t (m u) -> p m t u", u=PACK)
-            return (
-                (zg_first[:, :, m, :].rearrange("p u m t -> p m t u"), src[:, :, :, 0:1]),
-                (zg_rest[:, :, m, :].rearrange("p u m t -> p m t u"), src[:, :, :, 1:PACK]),
-            )
-
-        make_z(0, "z0")
-        z2_q = (
-            sb.tile([P, W], U32, name="z2_q", align_bytes=64),
-            sb.tile([P, W], U8, name="z2_qs", align_bytes=64),
-        )
+        z_low = make_z(0, "z0")
+        z2_q = mx_tiles("z2", W)
         for h in range(2):
             nc.vector.quantize_mx(
-                out=z2_q[0][:, cols(h)].bitcast(FP8X4), scales=z2_q[1][:, cols(h)], in_=z2_g[h][:]
+                out=z2_q[0][:, cols(h)].bitcast(FP8X4), scales=z2_q[1][:, cols(h)], in_=z2_grouped[h][:]
             )
-        zg_first = sb.tile([P, 1, P, PACK], BF16, name="zg_first", tag="z2p", align_bytes=64)
-        zg_rest = sb.tile([P, PACK - 1, P, PACK], BF16, name="zg_rest", tag="z2_g0", align_bytes=64)
-        for dst, src in z_views(0):
-            nc.scalar.copy(dst, src)
-        make_z(1, "z2_g1")
-        half_copy = {u: sb.tile([P, W], F32, name="hcv%d" % u) for u in TURNED}
-        half_cv = [half_copy[u][:] if u in TURNED else cv_w[u][:, :W] for u in range(PACK)]
-        accs = []
-        banks = 0
-        for u in range(PACK):
-            grouped = zg_first[:, 0] if u == 0 else zg_rest[:, u - 1]
-            nc.vector.tensor_copy(
-                grouped[:, P // 2 :, :], z[1][:].rearrange("p t (m u) -> p u m t", u=PACK)[:, u]
-            )
-            z_q = quantize("zrow%d" % u, grouped.rearrange("p m t -> p (m t)"), P)
-            accs.append([])
-            for c in [cols(0), cols(1)] if u == 0 else [slice(0, W)]:
-                acc = product(banks, z_q, slice(0, P), z2_q, c)
-                banks = banks + 1
-                nc.scalar.activation(cv_w[u][:, c], acc[:], COPY, scale=0.03125)
-                accs[u].append((acc, c))
-            if u in TURNED:
-                nc.scalar.activation(half_cv[u], acc[:], COPY, scale=0.03125)
 
-        res = [sb.tile([P, W], F32, name="res%d" % u) for u in range(PACK)]
-        diff = {u: sb.tile([P, W], F32, name="diff%d" % u) for u in TURNED}
+        z_first = sb.tile([P, 1, P, PACK], BF16, name="z_first", tag="z2_rows", align_bytes=64)
+        z_rest = sb.tile([P, PACK - 1, P, PACK], BF16, name="z_rest", tag="z2_grouped0", align_bytes=64)
+        z_grouped = [z_first[:, 0]] + [z_rest[:, u] for u in range(PACK - 1)]
+        low, high = slice(0, P // 2), slice(P // 2, P)
+        z_low_dealt = z_low[:].rearrange("p t (m u) -> p m t u", u=PACK)
+        nc.scalar.copy(z_first[:, :, low, :].rearrange("p u m t -> p m t u"), z_low_dealt[:, :, :, 0:1])
+        nc.scalar.copy(z_rest[:, :, low, :].rearrange("p u m t -> p m t u"), z_low_dealt[:, :, :, 1:PACK])
+        z_high = make_z(1, "z2_grouped1")
+
+        nc.scalar.copy(
+            z_rest[:, 1:, high, :].rearrange("p u m t -> p m t u"),
+            z_high[:].rearrange("p t (m u) -> p m t u", u=PACK)[:, :, :, 2:],
+        )
+
+        half_cv = [cv_w[u][:, :W] for u in range(PACK)]
+        cv_sums = []
+        for u in range(PACK):
+            if u < 2:
+                nc.vector.tensor_copy(
+                    z_grouped[u][:, high, :], z_high[:].rearrange("p t (m u) -> p u m t", u=PACK)[:, u]
+                )
+            z_q = quantize("z_tile%d" % u, z_grouped[u].rearrange("p m t -> p (m t)"), P)
+            for piece in [cols(0), cols(1)] if u == 0 else [whole]:
+                acc = product(len(cv_sums), z_q, slice(0, P), z2_q, piece)
+                nc.scalar.activation(cv_w[u][:, piece], acc[:], COPY, scale=0.03125)
+                cv_sums.append(acc)
+        cv_bank = {u: cv_sums[u + 1] for u in range(1, PACK)}
+
+        def hop(u):
+            factor = -1.0 if u in TURNED else 2.0
+            nc.vector.tensor_scalar(hopped[u], cv_w[u][:].indirect(n4_sb[:]), factor, 0.0, MULT, ADD)
+
+        def larger(u):
+            nc.vector.scalar_tensor_tensor(st_w[u][:, :W], cv_bank[u][:], 0.0625, hopped[u], MULT, MAX)
 
         def turn(bank, terms, dst, func, scale):
             acc = psum.tile([P, W], F32, name="turned", tag="bank%d" % bank)
-            steps = [(src, c) for src in terms for c in range(W // P)]
-            for i, (src, c) in enumerate(steps):
+            steps = [(term, c) for term in terms for c in range(W // P)]
+            for i, (term, c) in enumerate(steps):
                 block = slice(c * P, (c + 1) * P)
                 nc.tensor.matmul(
-                    acc[:, block], src[:, block], ident[:], is_transpose=True, start=i == 0, stop=i == len(steps) - 1
+                    acc[:, block], term[:, block], ident[:], is_transpose=True, start=i == 0, stop=i == len(steps) - 1
                 )
             nc.scalar.activation(dst, acc[:], func, scale=scale)
 
-        def hop(u):
-            if u in TURNED:
-                nc.vector.tensor_tensor(diff[u][:], cv_w[u][:].indirect(n4_sb[:]), half_cv[u], SUB)
-            else:
-                nc.vector.tensor_scalar(hopped[u], cv_w[u][:].indirect(n4_sb[:]), 2.0, 0.0, MULT, ADD)
+        def finish(u, result, pieces):
+            for offsets, piece in pieces:
+                nc.vector.tensor_tensor(result[:, piece], st_w[u][:].indirect(offsets), half_cv[u][:, piece], SUB)
+                nc.sync.dma_start(out_rows[u][:, piece], result[:, piece])
 
-        def larger(u):
-            for acc, c in accs[u]:
-                nc.vector.scalar_tensor_tensor(st_w[u][:, c], acc[:], 0.0625, hopped[u][:, c], MULT, MAX)
+        results = [sb.tile([P, W], F32, name="result%d" % u) for u in range(PACK - 1)]
+        for u in range(PACK):
+            hop(u)
+        larger(2)
 
-        def finish(u, pieces):
-            if pieces == 1:
-                nc.vector.tensor_tensor(res[u][:], st_w[u][:].indirect(n5_sb[:]), half_cv[u], SUB)
-                nc.sync.dma_start(out_rows[u], res[u][:])
-            else:
-                for h in range(2):
-                    nc.vector.tensor_tensor(
-                        res[u][:, cols(h)], st_w[u][:].indirect(entries(n5_sb, h)), half_cv[u][:, cols(h)], SUB
-                    )
-                    nc.sync.dma_start(out_rows[u][:, cols(h)], res[u][:, cols(h)])
+        half_turned = {u: sb.tile([P, W], F32, name="half_turned%d" % u) for u in TURNED}
+        excess_turned = {u: sb.tile([P, W], F32, name="excess_turned%d" % u) for u in TURNED}
 
-        hop(0)
-        hop(1)
-        larger(0)
-        hop(2)
-        hop(3)
-        half_t = {u: sb.tile([P, W], F32, name="half_t%d" % u) for u in TURNED}
-        gain_t = {u: sb.tile([P, W], F32, name="gain_t%d" % u) for u in TURNED}
-        for u, bank in zip(TURNED, (5, 6)):
-            turn(bank, [half_cv[u]], half_t[u][:], COPY, 1.0)
-        for u, bank in zip(TURNED, (7, 2)):
-            turn(bank, [diff[u][:]], gain_t[u][:], RELU, 1.0)
-        for u, bank in zip(TURNED, (3, 5)):
-            turn(bank, [half_t[u][:], gain_t[u][:]], st_w[u][:, :W], COPY, 2.0)
-        finish(0, 1)
+        def turn_half(u, bank):
+            turn(bank, [half_cv[u]], half_turned[u][:], COPY, 1.0)
+
+        def turn_excess(u, bank):
+            turn(bank, [half_cv[u], hopped[u]], excess_turned[u][:], RELU, -1.0)
+
+        def turn_back(u, bank):
+            turn(bank, [half_turned[u][:], excess_turned[u][:]], st_w[u][:, :W], COPY, 2.0)
+
+        turn_half(0, 5)
+        turn_excess(0, 6)
+        turn_half(1, 7)
+        turn_back(0, 0)
+        turn_excess(1, 1)
+        turn_back(1, 2)
+
+        in_one = [(n5_sb[:], whole)]
+        in_halves = [(entries(n5_sb, h), cols(h)) for h in range(2)]
+        finish(2, results[2], in_one)
         larger(3)
-        finish(3, 1)
-        finish(1, 1)
-        finish(2, 2)
+        finish(0, results[0], in_one)
+        last_result = sb.tile([P, W], F32, name="result3", tag="excess_turned1")
+        finish(3, last_result, in_one)
+        finish(1, results[1], in_halves)

from contextlib import ExitStack

import concourse.mybir as mybir
from concourse.masks import make_identity

K, T, S, H, N = 512, 2048, 512, 512, 512
FLOPS = 2 * K * S * H + 2 * K * S * N + 2 * S * H * N

F32 = mybir.dt.float32
BF16 = mybir.dt.bfloat16
I32 = mybir.dt.int32
U32 = mybir.dt.uint32
U16 = mybir.dt.uint16
U8 = mybir.dt.uint8
FP8X4 = mybir.dt.float8_e4m3fn_x4
COPY = mybir.ActivationFunctionType.Copy
RELU = mybir.ActivationFunctionType.Relu
MULT = mybir.AluOpType.mult
ADD = mybir.AluOpType.add
SUB = mybir.AluOpType.subtract
MAX = mybir.AluOpType.max

P = 128
PACK = 4
W = 512
HALF = W // 2
STRIPE = 16
QUADRANT = 32
TURNED = (0, 1)


def tile_picked_momkindahopb_none_p_kernel(
    tc, x_words, x_scales, wa, wb, tab, gt, gi, offs, two, n1, n2, n3, n4, n5, out
):
    nc = tc.nc
    with ExitStack() as ctx:
        lists = ctx.enter_context(tc.tile_pool(name="lists", bufs=1))
        sb = ctx.enter_context(tc.tile_pool(name="sb", bufs=1))
        psum = ctx.enter_context(tc.psum_pool(name="psum", bufs=1))

        def cols(h):
            return slice(h * HALF, (h + 1) * HALF)

        def entries(list_tile, h):
            return list_tile[:, h * HALF // STRIPE : (h + 1) * HALF // STRIPE]

        def wide_tiles(name, row_tiles):
            return {t: sb.tile([P, 2 * W], F32, name="%s%d" % (name, t)) for t in row_tiles}

        tab_w = wide_tiles("tab_w", range(PACK))
        a_w = wide_tiles("a_w", (0, 1, 3))
        cv_w = wide_tiles("cv_w", range(PACK))
        st_w = wide_tiles("st_w", range(PACK))
        tab_n1 = [a_w[(t - 1) % PACK][:, W:] for t in range(PACK - 1)]
        prod = [cv_w[t][:, W:] for t in range(PACK)]
        hopped = [st_w[u][:, W:] for u in range(PACK)]

        tab_rows = tab.rearrange("(p t) j -> t p j", t=PACK)
        out_rows = out.rearrange("(p u) j -> u p j", u=PACK)

        def load_list(name, src):
            list_tile = lists.tile([P, W // STRIPE], U16, name=name)
            nc.sync.dma_start(list_tile[:], src)
            return list_tile

        def load_tab(t):
            nc.sync.dma_start(tab_w[t][:, :W], tab_rows[t])

        def load_weight(name, src, h):
            raw = sb.tile([P, PACK, HALF], F32, name="%s_raw%d" % (name, h))
            nc.sync.dma_start(raw[:], src.rearrange("(p t) c -> p t c", t=PACK)[:, :, cols(h)])
            return raw

        def load_gain(name, src):
            gain = sb.tile([P, PACK], F32, name=name)
            nc.gpsimd.dma_start(gain[:], src.rearrange("(p t) o -> p (t o)", t=PACK))
            return gain

        xs = sb.tile([P, T], U8, name="xs", align_bytes=64)
        nc.vector.memset(xs[:].bitcast(I32), 0)
        nc.vector.memset(tab_w[0][:, W:], 0.0)
        nc.vector.memset(tab_w[1][:, W:], 0.0)
        nc.gpsimd.memset(tab_w[2][:, W:], 0.0)
        gt_sb = load_gain("gt", gt)
        nc.gpsimd.memset(tab_w[3][:, W:], 0.0)
        gi_sb = load_gain("gi", gi)
        ident = sb.tile([P, P], F32, name="ident")
        make_identity(nc, ident[:])

        load_tab(0)
        n1_sb = load_list("n1", n1)
        load_tab(1)
        load_tab(2)
        xw = sb.tile([P, T], I32, name="xw", align_bytes=64)
        nc.sync.dma_start(xw[:], x_words[0].rearrange("p n t -> p (n t)").bitcast(I32))
        for q in range(P // QUADRANT):
            nc.scalar.dma_start(
                xs[QUADRANT * q : QUADRANT * q + 4, :].bitcast(I32), x_scales[0, 4 * q : 4 * q + 4, :].bitcast(I32)
            )
        offs_sb = load_list("offs", offs)
        wa_raw = [load_weight("wa", wa, h) for h in range(2)]
        two_sb = load_list("two", two)
        wb_raw = [load_weight("wb", wb, h) for h in range(2)]
        load_tab(3)
        n3_sb = load_list("n3", n3)
        n2_sb = load_list("n2", n2)
        n4_sb = load_list("n4", n4)
        n5_sb = load_list("n5", n5)

        def gather_tab_n1(t):
            nc.vector.tensor_copy(tab_n1[t], tab_w[t][:].indirect(n1_sb[:]))

        def pick_words(name, list_tile):
            words = sb.tile([P, S], U32, name=name + "_words", align_bytes=64)
            nc.vector.tensor_copy(
                words[:].rearrange("p (t m) -> p m t", t=PACK), xw[:].bitcast(U32).indirect(list_tile[:])
            )
            return words

        def pick_scales(name, list_tile, tag):
            picked = sb.tile([P, S], U8, name=name + "_picked", tag=tag, align_bytes=64)
            nc.vector.tensor_copy(picked[:], xs[:].indirect(list_tile[:]))
            dealt = sb.tile([P, S], U8, name=name + "_dealt", align_bytes=64)
            nc.vector.tensor_copy(
                dealt[:].rearrange("p (t b i) -> p b t i", t=PACK, i=16),
                picked[:].rearrange("p (b i t) -> p b t i", t=PACK, i=16),
            )
            return dealt

        def interleave(grouped, row_tiles):
            nc.scalar.copy(
                grouped.rearrange("p (c i t) -> p c t i", t=PACK, i=4),
                row_tiles.rearrange("p t (c i) -> p c t i", i=4),
            )

        def interleave_weight(name, raw):
            grouped = sb.tile([P, PACK * W], BF16, name=name + "_grouped", align_bytes=64)
            for h in range(2):
                interleave(grouped[:, h * PACK * HALF : (h + 1) * PACK * HALF], raw[h][:])
            return grouped

        def mx_tiles(name, width):
            codes = sb.tile([P, width], U32, name=name + "_codes", align_bytes=64)
            scales = sb.tile([P, width], U8, name=name + "_scales", align_bytes=64)
            return codes, scales

        def quantize(name, grouped, width):
            codes, scales = mx_tiles(name, width)
            nc.vector.quantize_mx(out=codes[:].bitcast(FP8X4), scales=scales[:], in_=grouped)
            return codes, scales

        def product(bank, lhs, lhs_cols, rhs, rhs_cols):
            acc = psum.tile([P, rhs_cols.stop - rhs_cols.start], F32, name="acc", tag="bank%d" % bank)
            nc.tensor.matmul_mx(
                out=acc[:],
                lhsT=lhs[0][:, lhs_cols].bitcast(FP8X4),
                lhsT_scale=lhs[1][:, lhs_cols],
                rhs=rhs[0][:, rhs_cols].bitcast(FP8X4),
                rhs_scale=rhs[1][:, rhs_cols],
                start=True,
                stop=True,
            )
            return acc

        whole = slice(0, W)
        tab_gt = [sb.tile([P, W], F32, name="tab_gt%d" % t) for t in range(PACK)]

        def scale_tab(t):
            nc.scalar.activation(tab_gt[t][:], tab_w[t][:, :W], COPY, scale=gt_sb[:, t : t + 1])

        for t in range(PACK - 1):
            gather_tab_n1(t)
            scale_tab(t)
        wa_grouped = interleave_weight("wa", wa_raw)
        xa = pick_words("xa", offs_sb), pick_scales("xa", offs_sb, "xa_picked")
        xb_words = pick_words("xb", two_sb)
        wa_q = quantize("wa", wa_grouped[:], W)
        xb = xb_words, pick_scales("xb", two_sb, "wa_grouped")
        wb_grouped = interleave_weight("wb", wb_raw)
        wb_q = quantize("wb", wb_grouped[:], W)
        a_w[2] = sb.tile([P, 2 * W], F32, name="a_w2", tag="wb_grouped", align_bytes=64)
        tab_n1.append(a_w[2][:, W:])
        gather_tab_n1(3)
        for t in range(PACK):
            acc = product(t, xa, slice(t * P, (t + 1) * P), wa_q, whole)
            nc.scalar.activation(a_w[t][:, :W], acc[:], COPY, scale=gt_sb[:, t : t + 1])
        scale_tab(3)

        z2_rows = sb.tile([P, PACK, W], BF16, name="z2_rows", align_bytes=64)
        for t in range(PACK):
            acc = product(PACK + t, xb, slice(t * P, (t + 1) * P), wb_q, whole)
            nc.scalar.activation(z2_rows[:, t, :], acc[:], COPY, scale=gi_sb[:, t : t + 1])
        z2_grouped = [sb.tile([P, PACK * HALF], BF16, name="z2_grouped%d" % h, align_bytes=64) for h in range(2)]
        for h in range(2):
            interleave(z2_grouped[h][:], z2_rows[:, :, cols(h)])

        for t in range(PACK):
            nc.vector.tensor_tensor(prod[t], a_w[t][:].indirect(n3_sb[:]), tab_n1[t], MULT)

        def make_z(h, tag):
            z_half = sb.tile([P, PACK, HALF], F32, name="z%d" % h, tag=tag, align_bytes=64)
            for t in range(PACK):
                nc.vector.tensor_tensor(
                    z_half[:, t, :], tab_gt[t][:].indirect(entries(n2_sb, h)), prod[t][:, cols(h)], ADD
                )
            return z_half

        z_low = make_z(0, "z0")
        z2_q = mx_tiles("z2", W)
        for h in range(2):
            nc.vector.quantize_mx(
                out=z2_q[0][:, cols(h)].bitcast(FP8X4), scales=z2_q[1][:, cols(h)], in_=z2_grouped[h][:]
            )

        z_first = sb.tile([P, 1, P, PACK], BF16, name="z_first", tag="z2_rows", align_bytes=64)
        z_rest = sb.tile([P, PACK - 1, P, PACK], BF16, name="z_rest", tag="z2_grouped0", align_bytes=64)
        z_grouped = [z_first[:, 0]] + [z_rest[:, u] for u in range(PACK - 1)]
        low, high = slice(0, P // 2), slice(P // 2, P)
        z_low_dealt = z_low[:].rearrange("p t (m u) -> p m t u", u=PACK)
        nc.scalar.copy(z_first[:, :, low, :].rearrange("p u m t -> p m t u"), z_low_dealt[:, :, :, 0:1])
        nc.scalar.copy(z_rest[:, :, low, :].rearrange("p u m t -> p m t u"), z_low_dealt[:, :, :, 1:PACK])
        z_high = make_z(1, "z2_grouped1")

        nc.scalar.copy(
            z_rest[:, 1:, high, :].rearrange("p u m t -> p m t u"),
            z_high[:].rearrange("p t (m u) -> p m t u", u=PACK)[:, :, :, 2:],
        )

        half_cv = [cv_w[u][:, :W] for u in range(PACK)]
        cv_sums = []
        for u in range(PACK):
            if u < 2:
                nc.vector.tensor_copy(
                    z_grouped[u][:, high, :], z_high[:].rearrange("p t (m u) -> p u m t", u=PACK)[:, u]
                )
            z_q = quantize("z_tile%d" % u, z_grouped[u].rearrange("p m t -> p (m t)"), P)
            for piece in [cols(0), cols(1)] if u == 0 else [whole]:
                acc = product(len(cv_sums), z_q, slice(0, P), z2_q, piece)
                nc.scalar.activation(cv_w[u][:, piece], acc[:], COPY, scale=0.03125)
                cv_sums.append(acc)
        cv_bank = {u: cv_sums[u + 1] for u in range(1, PACK)}

        def hop(u):
            factor = -1.0 if u in TURNED else 2.0
            nc.vector.tensor_scalar(hopped[u], cv_w[u][:].indirect(n4_sb[:]), factor, 0.0, MULT, ADD)

        def larger(u):
            nc.vector.scalar_tensor_tensor(st_w[u][:, :W], cv_bank[u][:], 0.0625, hopped[u], MULT, MAX)

        def turn(bank, terms, dst, func, scale):
            acc = psum.tile([P, W], F32, name="turned", tag="bank%d" % bank)
            steps = [(term, c) for term in terms for c in range(W // P)]
            for i, (term, c) in enumerate(steps):
                block = slice(c * P, (c + 1) * P)
                nc.tensor.matmul(
                    acc[:, block], term[:, block], ident[:], is_transpose=True, start=i == 0, stop=i == len(steps) - 1
                )
            nc.scalar.activation(dst, acc[:], func, scale=scale)

        def finish(u, result, pieces):
            for offsets, piece in pieces:
                nc.vector.tensor_tensor(result[:, piece], st_w[u][:].indirect(offsets), half_cv[u][:, piece], SUB)
                nc.sync.dma_start(out_rows[u][:, piece], result[:, piece])

        results = [sb.tile([P, W], F32, name="result%d" % u) for u in range(PACK - 1)]
        for u in range(PACK):
            hop(u)
        larger(2)

        half_turned = {u: sb.tile([P, W], F32, name="half_turned%d" % u) for u in TURNED}
        excess_turned = {u: sb.tile([P, W], F32, name="excess_turned%d" % u) for u in TURNED}

        def turn_half(u, bank):
            turn(bank, [half_cv[u]], half_turned[u][:], COPY, 1.0)

        def turn_excess(u, bank):
            turn(bank, [half_cv[u], hopped[u]], excess_turned[u][:], RELU, -1.0)

        def turn_back(u, bank):
            turn(bank, [half_turned[u][:], excess_turned[u][:]], st_w[u][:, :W], COPY, 2.0)

        turn_half(0, 5)
        turn_excess(0, 6)
        turn_half(1, 7)
        turn_back(0, 0)
        turn_excess(1, 1)
        turn_back(1, 2)

        in_one = [(n5_sb[:], whole)]
        in_halves = [(entries(n5_sb, h), cols(h)) for h in range(2)]
        finish(2, results[2], in_one)
        larger(3)
        finish(0, results[0], in_one)
        last_result = sb.tile([P, W], F32, name="result3", tag="excess_turned1")
        finish(3, last_result, in_one)
        finish(1, results[1], in_halves)
